import numpy as np
import ml_dtypes


def mxq(x, axis, fmt="e4m3"):
    dtype, down = {"e4m3": (ml_dtypes.float8_e4m3fn, 7), "e5m2": (ml_dtypes.float8_e5m2, 14)}[fmt]
    v = np.moveaxis(np.asarray(x, np.float32).astype(ml_dtypes.bfloat16).astype(np.float64), axis, -1)
    blocks = v.reshape(v.shape[:-1] + (-1, 32))
    amax = np.abs(blocks).max(-1, keepdims=True)
    byte = np.maximum(np.where(amax > 0, np.frexp(amax)[1] - 1 + 127, 0) - down, 1)
    scale = np.exp2(byte - 127.0)
    codes = (blocks / scale).astype(np.float32).astype(dtype).astype(np.float64)
    return np.moveaxis((codes * scale).reshape(v.shape), -1, axis)


WIDE = False


def mx_kscale(k):
    if not WIDE:
        return np.ones(k)
    levels = np.array([10, -10, 5, -5, 0])
    if k % 512:
        return np.exp2(np.random.permutation(np.resize(levels, k // 32))).repeat(32)
    a = np.empty((k // 512, 16))
    for p in range(k // 512):
        a[p, :8] = np.random.permutation(np.resize(levels, 8))
        for g in range(8):
            far = levels[np.abs(levels - a[p, g]) >= 10]
            a[p, g + 8] = far[np.random.randint(len(far))]
    return np.exp2(a.ravel()).repeat(32)


BF16 = ml_dtypes.bfloat16


def bf(x):
    return np.asarray(x, np.float32).astype(BF16)


def f64(x):
    return np.asarray(x).astype(np.float64)


E2M1 = np.array([0.0, 0.5, 1.0, 1.5, 2.0, 3.0, 4.0, 6.0, -0.0, -0.5, -1.0, -1.5, -2.0, -3.0, -4.0, -6.0])


def pack_weight(w, fmt):
    k, n = w.shape
    w = f64(bf(w)).reshape(k // 32, 32, n)
    amax = np.abs(w).max(1)
    if fmt == "e4m3":
        byte = np.frexp(amax)[1] - 1 + 127 - 7
    else:
        mant, ex = np.frexp(amax / 6.0)
        byte = np.where(mant > 0.5, ex, ex - 1) + 127
    byte = np.clip(np.where(amax > 0, byte, 1), 1, 254)
    scaled = (w * np.exp2(127.0 - byte)[:, None, :]).reshape(k, n).astype(np.float32)
    by_word = np.ascontiguousarray(scaled.reshape(k // 512, 128, 4, n).transpose(0, 1, 3, 2))
    if fmt == "e4m3":
        words = by_word.astype(ml_dtypes.float8_e4m3fn).view(np.uint8)
    else:
        c = by_word.astype(ml_dtypes.float4_e2m1fn).view(np.uint8) & 0xF
        words = c[..., 0::2] | (c[..., 1::2] << 4)
    return np.ascontiguousarray(words), np.ascontiguousarray(byte.astype(np.uint8).reshape(k // 512, 16, n))


def unpack_weight(words, scales, fmt):
    g, p, n, _ = words.shape
    if fmt == "e4m3":
        vals = np.ascontiguousarray(words).view(ml_dtypes.float8_e4m3fn).astype(np.float64)
    else:
        nib = np.empty((g, p, n, 4), np.uint8)
        nib[..., 0::2] = words & 0xF
        nib[..., 1::2] = words >> 4
        vals = E2M1[nib]
    vals = vals * np.repeat(np.exp2(scales.astype(np.float64) - 127.0), 8, axis=1)[..., None]
    return vals.transpose(0, 1, 3, 2).reshape(g * 512, n)
def pack4(w):
    words, scales = pack_weight(w, "e2m1")
    return words.reshape(words.shape[0], 128, -1), scales


def unpack4(words, scales):
    return unpack_weight(words.reshape(words.shape[0], 128, -1, 2), scales, "e2m1")


E4M3FN = np.array([(-1.0 if i & 128 else 1.0) * ((1.0 + (i & 7) / 8.0) * 2.0 ** (((i >> 3) & 15) - 7) if i & 120 else (i & 7) * 2.0 ** -9) for i in range(256)])


def e4m3fn_bytes(y):
    return np.clip(np.asarray(y, np.float64), -448.0, 448.0).astype(np.float32).astype(ml_dtypes.float8_e4m3fn).view(np.uint8)


def e4m3fn_values(b):
    return E4M3FN[b]


U, I, F, H, B = 1024, 3072, 1024, 1024, 128


def setup_inputs():
    s, t = mx_kscale(I), mx_kscale(F)
    c = np.random.exponential(1.0, (U, I))
    x = c / np.sqrt((c * c).sum(axis=1, keepdims=True)) * s
    x_scale = (np.abs(x).reshape(U, I // B, B).max(axis=2) / 448).astype(np.float32)
    w1_words, w1_scales = pack4(np.random.standard_normal((I, F)) / s[:, None] * t)
    w2 = np.random.standard_normal((H, F)) / np.sqrt(F) / t
    w2_scale = (np.abs(w2).reshape(H // B, B, F // B, B).max(axis=(1, 3)) / 448).astype(np.float32)
    return {"x_bytes": e4m3fn_bytes(x / np.repeat(f64(x_scale), B, axis=1)),
            "x_scale": x_scale,
            "w1_words": w1_words,
            "w1_scales": w1_scales,
            "b1": bf(0.3 * np.random.standard_normal(F) * t),
            "w2_bytes": e4m3fn_bytes(w2 / np.repeat(np.repeat(f64(w2_scale), B, axis=0), B, axis=1)),
            "w2_scale": w2_scale,
            "b2": bf(0.3 * np.random.standard_normal(H))}


def reference(x_bytes, x_scale, w1_words, w1_scales, b1, w2_bytes, w2_scale, b2):
    x = e4m3fn_values(x_bytes) * np.repeat(f64(x_scale), B, axis=1)
    w2 = e4m3fn_values(w2_bytes) * np.repeat(np.repeat(f64(w2_scale), B, axis=0), B, axis=1)
    a = mxq(x, 1, "e4m3") @ unpack4(w1_words, w1_scales)
    h = np.maximum(a + f64(b1), 0.0)
    y = mxq(h, 1, "e4m3") @ mxq(w2, 1, "e4m3").T
    return np.tanh(y + f64(b2))

@@ -1,0 +1,462 @@
+from contextlib import ExitStack
+
+import concourse.mybir as mybir
+from concourse.masks import make_identity
+
+USERS, ITEMS, HIDDEN, CODES = 1024, 3072, 1024, 1024
+FLOPS = 2 * USERS * ITEMS * HIDDEN + 2 * USERS * HIDDEN * CODES
+
+F32 = mybir.dt.float32
+BF16 = mybir.dt.bfloat16
+I32 = mybir.dt.int32
+U32 = mybir.dt.uint32
+U8 = mybir.dt.uint8
+FP8 = mybir.dt.float8_e4m3fn
+FP8X4 = mybir.dt.float8_e4m3fn_x4
+FP4X4 = mybir.dt.float4_e2m1fn_x4
+ACT = mybir.ActivationFunctionType
+ALU = mybir.AluOpType
+
+P = 128
+PASS = 512
+X_PASSES = ITEMS // PASS
+H_PASSES = HIDDEN // PASS
+TILES = 4
+X_CHUNKS = [[(0, 1), (1, 2), (2, 4), (4, 6)], [(0, 2), (2, 4), (4, 6)]]
+W1_CHUNKS = [(0, 1), (1, 2), (2, 4), (4, 6)]
+WIDE_SLOTS = 8
+WOVEN_SLOTS = 4
+RESULT_SLOTS = 8
+
+
+def chunk_of(chunks, g):
+    return [c for c in chunks if c[0] <= g < c[1]][0]
+
+
+def engine_orders():
+    xa = [("x", 0, g) for g in range(X_PASSES)]
+    xb = [("x", 1, g) for g in range(X_PASSES)]
+    w2 = [("w", n, g) for n in range(2) for g in range(H_PASSES)]
+    stream = xa + xb + w2
+    bank_of = {}
+    tensor = []
+
+    def turn(unit, first_bank):
+        for pair in range(2):
+            bank_of[("empty", unit, pair)] = first_bank + pair
+            tensor.append(("turn", unit, pair))
+
+    def mm1(half, fs, gs):
+        tensor.extend(("mm1", half, f, g) for g in gs for f in fs)
+
+    def mm2(key, bank, gs):
+        bank_of[("bias", key)] = bank
+        tensor.extend(("mm2", key, g) for g in gs)
+
+    def warm(first, count):
+        for i in range(first, first + count):
+            bank_of[("warm_tensor", i)] = 1
+            tensor.append(("warm_tensor", i))
+
+    for f, bank in enumerate([0, 1, 2, 3, 4, 5, 0, 1]):
+        bank_of[("relu", 0, f)] = bank
+    for f, bank in enumerate([2, 3, 4, 5, 6, 2, 4, 6]):
+        bank_of[("relu", 1, f)] = bank
+    bank_of[("empty_b1",)] = 0
+    warm(0, 6)
+    tensor.append(("turn_b1",))
+    turn(xa[0], 6)
+    warm(10, 2)
+    turn(xa[1], 4)
+    warm(20, 1)
+    for g in range(X_PASSES):
+        mm1(0, range(6), [g])
+        turn(stream[g + 2], 6)
+    mm1(0, [6], range(X_PASSES))
+    turn(xb[2], 6)
+    mm1(0, [7], range(X_PASSES))
+    mm1(1, range(4), [0])
+    turn(xb[3], 6)
+    turn(xb[4], 0)
+    mm1(1, range(4), [1, 2])
+    turn(xb[5], 6)
+    turn(w2[0], 0)
+    mm1(1, range(4), [3, 4])
+    turn(w2[1], 6)
+    turn(w2[2], 0)
+    mm1(1, range(4), [5])
+    keys_a = [(0, a, n) for n in range(2) for a in range(TILES)]
+    keys_b = [(1, a, n) for a in range(TILES) for n in range(2)]
+    mm1(1, [4], range(X_PASSES))
+    turn(w2[3], 0)
+    mm2(keys_a[0], 7, range(2))
+    mm2(keys_a[1], 3, range(2))
+    mm1(1, [5], range(X_PASSES))
+    mm2(keys_a[2], 5, range(2))
+    mm2(keys_a[3], 7, range(2))
+    mm1(1, [6], range(X_PASSES))
+    mm2(keys_a[4], 0, range(2))
+    mm2(keys_a[5], 1, range(2))
+    mm1(1, [7], range(X_PASSES))
+    mm2(keys_a[6], 3, range(2))
+    mm2(keys_a[7], 5, range(2))
+    tail_banks = [7, 2, 0, 1, 4, 6, 3, 5]
+    for i, key in enumerate(keys_b[:4]):
+        mm2(key, tail_banks[i], [0])
+    for i, key in enumerate(keys_b[:4]):
+        mm2(key, tail_banks[i], [1])
+    for i, key in enumerate(keys_b[4:]):
+        mm2(key, tail_banks[4 + i], range(2))
+
+    def widen(unit, tiles):
+        return [("widen", unit, a) for a in tiles]
+
+    def empty(unit):
+        return [("empty", unit, 0), ("empty", unit, 1)]
+
+    helped = [0, 1, 2, 3]
+
+    def own(i):
+        return widen(stream[i], range(3) if i in helped else range(4))
+
+    def aid(i):
+        return widen(stream[i], [3]) if i in helped else []
+
+    whole = (0, TILES)
+    vector = [("fill_warm",), ("fill_b1",), ("fill_w1_scales",)]
+    vector += own(0) + [("empty_b1",), ("sort_words", W1_CHUNKS[0], 0)] + own(1) + [("sort_scales", 0), ("quant", xa[0])]
+    vector += [("sort_scales", 1), ("sort_words", W1_CHUNKS[0], 1)] + own(2)[:1] + [("quant", xa[1])] + own(2)[1:]
+    vector += [("sort_words", W1_CHUNKS[1], 0), ("sort_words", W1_CHUNKS[1], 1)]
+    vector += own(3) + [("sort_words", W1_CHUNKS[2], 0), ("quant", xa[2]), ("sort_words", W1_CHUNKS[2], 1)]
+    vector += own(4) + [("quant", xa[3])] + own(5) + [("sort_words", W1_CHUNKS[3], 0), ("quant", xa[4]), ("sort_words", W1_CHUNKS[3], 1)]
+    vector += own(6) + [("quant", xa[5])] + own(7) + own(8) + [("quant", xb[0])] + own(9) + own(10) + [("quant", xb[1])]
+    vector += own(11) + own(12) + [("quant", xb[2])] + own(13) + [("quant", xb[3]), ("h_weave", 0, 0, whole), ("quant", xb[4])]
+    vector += own(14) + [("quant", xb[5])] + own(15) + [("quant", w2[0]), ("h_quant", 0, 0, whole), ("h_quant", 0, 1, whole), ("quant", w2[1]), ("quant", w2[2])]
+    vector += [("h_weave", 1, 0, whole), ("quant", w2[3])] + [("bias", key) for key in keys_a[:2]] + [("h_quant", 1, 0, whole)]
+    vector += [("bias", key) for key in keys_a[2:6]]
+    vector += [("h_weave", 1, 1, (0, 1)), ("h_weave", 1, 1, (1, 2)), ("h_quant", 1, 1, (0, 1)), ("h_weave", 1, 1, (2, 3)), ("h_quant", 1, 1, (1, 2)), ("bias", keys_a[6]), ("h_quant", 1, 1, (2, 4)), ("bias", keys_a[7])]
+    vector += [("bias", key) for key in keys_b]
+
+    scalar = [("warm_scalar",)] + aid(0) + [("empty", xa[0], 0)] + aid(1) + [("empty", xa[0], 1)] + empty(xa[1]) + aid(2)
+    for i in range(2, 8):
+        scalar += aid(i + 1) + empty(stream[i]) if i < 7 else []
+    scalar += [("relu", 0, 0), ("relu", 0, 1)] + empty(xb[1]) + [("relu", 0, f) for f in range(2, 5)] + empty(xb[2]) + [("relu", 0, f) for f in range(5, 8)] + empty(xb[3]) + empty(xb[4])
+    scalar += [("h_weave", 0, 1, (0, 2))] + empty(xb[5]) + empty(w2[0]) + [("h_weave", 0, 1, (2, 4))] + empty(w2[1]) + empty(w2[2])
+    scalar += [("relu", 1, f) for f in range(4)] + empty(w2[3])
+    scalar += [("relu", 1, 4)] + [("tanh", key) for key in keys_a[:2]] + [("relu", 1, 5), ("tanh", keys_a[2]), ("tanh", keys_a[3]), ("relu", 1, 6), ("tanh", keys_a[4]), ("tanh", keys_a[5]), ("relu", 1, 7), ("h_weave", 1, 1, (3, 4))]
+    scalar += [("tanh", key) for key in keys_a[6:] + keys_b]
+
+    sync = [("load_x_scale",), ("load_x", 0, X_CHUNKS[0][0]), ("load_b1",), ("load_w1", W1_CHUNKS[0]), ("load_x", 0, X_CHUNKS[0][1]), ("load_w1_scales",)]
+    sync += [("load_x", 0, X_CHUNKS[0][2]), ("load_w1", W1_CHUNKS[1]), ("load_w1", W1_CHUNKS[2]), ("load_x", 0, X_CHUNKS[0][3]), ("load_w1", W1_CHUNKS[3])]
+    sync += [("load_x", 1, c) for c in X_CHUNKS[1]] + [("load_w2_scale",), ("load_w2", 0), ("load_w2", 1), ("load_b2",)]
+    sync += [("store", key) for key in keys_a + keys_b]
+    return {"sync": sync, "gpsimd": [("fill_zeros",), ("identities",)], "vector": vector, "scalar": scalar, "tensor": tensor}, bank_of
+
+
+def prerequisites(orders):
+    needs = {}
+    steps = [step for order in orders.values() for step in order]
+    units = [step[1] for step in orders["tensor"] if step[0] == "turn" and step[2] == 0]
+    results = [step[1] for step in orders["vector"] if step[0] == "bias"]
+    parts = {}
+    for step in steps:
+        if step[0] == "h_quant":
+            parts.setdefault(step[1:3], []).append(step[3])
+    for step in steps:
+        kind = step[0]
+        before = []
+        if kind == "widen":
+            unit, a = step[1], step[2]
+            if unit[0] == "x":
+                before += [("load_x", unit[1], chunk_of(X_CHUNKS[unit[1]], unit[2])), ("load_x_scale",)]
+            else:
+                before += [("load_w2", unit[1]), ("load_w2_scale",)]
+            if units.index(unit) >= WIDE_SLOTS:
+                before.append(("turn", units[units.index(unit) - WIDE_SLOTS], a // 2))
+        elif kind == "turn":
+            before += [("widen", step[1], 2 * step[2]), ("widen", step[1], 2 * step[2] + 1), ("identities",)]
+        elif kind == "empty":
+            before.append(("turn", step[1], step[2]))
+            if units.index(step[1]) >= WOVEN_SLOTS:
+                before.append(("quant", units[units.index(step[1]) - WOVEN_SLOTS]))
+        elif kind == "quant":
+            before += [("empty", step[1], 0), ("empty", step[1], 1)]
+        elif kind == "load_w1_scales":
+            before.append(("fill_w1_scales",))
+        elif kind == "warm_tensor":
+            before.append(("fill_zeros",))
+        elif kind == "warm_scalar":
+            before.append(("fill_warm",))
+        elif kind == "load_b1":
+            before.append(("fill_b1",))
+        elif kind == "sort_words":
+            before.append(("load_w1", step[1]))
+        elif kind == "sort_scales":
+            before.append(("load_w1_scales",))
+        elif kind == "turn_b1":
+            before += [("load_b1",), ("identities",)]
+        elif kind == "empty_b1":
+            before.append(("turn_b1",))
+        elif kind == "mm1":
+            half, f, g = step[1:4]
+            before += [("quant", ("x", half, g)), ("sort_words", chunk_of(W1_CHUNKS, g), f // 4), ("sort_scales", f // 4)]
+        elif kind == "relu":
+            before += [("mm1", step[1], step[2], X_PASSES - 1), ("empty_b1",)]
+        elif kind == "h_weave":
+            before += [("relu", step[1], 4 * step[2] + t) for t in range(4)]
+        elif kind == "h_quant":
+            before += [s for s in steps if s[:3] == ("h_weave",) + step[1:3] and s[3][0] < step[3][1] and step[3][0] < s[3][1]]
+        elif kind == "mm2":
+            (half, a, n), g = step[1], step[2]
+            before.append(("quant", ("w", n, g)))
+            before += [("h_quant", half, g, part) for part in parts[(half, g)] if part[0] <= a < part[1]]
+        elif kind == "bias":
+            before += [("mm2", step[1], H_PASSES - 1), ("load_b2",)]
+            if results.index(step[1]) >= RESULT_SLOTS:
+                before.append(("store", results[results.index(step[1]) - RESULT_SLOTS]))
+        elif kind == "tanh":
+            before.append(("bias", step[1]))
+        elif kind == "store":
+            before.append(("tanh", step[1]))
+        needs[step] = before
+    return needs, units, results
+
+
+def tile_click_autoencoder_encoder_d6_kernel(
+    tc, x_bytes, x_scale, w1_words, w1_scales, b1, w2_bytes, w2_scale, b2, out
+):
+    nc = tc.nc
+    orders, bank_of = engine_orders()
+    needs, units, results = prerequisites(orders)
+    engine_of = {step: engine for engine, order in orders.items() for step in order}
+
+    emptied_by = {}
+    for step in orders["tensor"]:
+        tenant = {"turn": ("empty",) + step[1:], "turn_b1": ("empty_b1",), "mm1": ("relu",) + step[1:3], "mm2": ("bias",) + step[1:2]}.get(step[0])
+        if tenant is None:
+            continue
+        bank = bank_of[tenant]
+        if emptied_by.get(bank, tenant) != tenant:
+            needs[step].append(emptied_by[bank])
+        emptied_by[bank] = tenant
+
+    with ExitStack() as ctx:
+        sbuf = ctx.enter_context(tc.tile_pool(name="sbuf", bufs=1))
+        psum = ctx.enter_context(tc.psum_pool(name="psum", bufs=1))
+
+        def alloc(name, shape, dtype):
+            return sbuf.tile(shape, dtype, name=name, align_bytes=64)
+
+        banks = [psum.tile([P, PASS], F32, name="bank%d" % b) for b in range(8)]
+        x_raw = {
+            (half, c): alloc("x_raw%d_%d" % (half, c[0]), [P, TILES, (c[1] - c[0]) * PASS], U8)
+            for half in range(2)
+            for c in X_CHUNKS[half]
+        }
+        w2_raw = [alloc("w2_raw%d" % n, [P, TILES, HIDDEN], U8) for n in range(2)]
+        x_sc = alloc("x_sc", [P, 2 * TILES * (ITEMS // P)], F32)
+        w2_sc = alloc("w2_sc", [P, 64], F32)
+        w1_raw = {c: alloc("w1_raw%d" % c[0], [P, c[1] - c[0], 2 * HIDDEN], U8) for c in W1_CHUNKS}
+        w1_sorted = alloc("w1_sorted", [P, X_PASSES, 2 * HIDDEN], U8)
+        w1s_raw = alloc("w1s_raw", [P, X_PASSES, HIDDEN], U8)
+        w1s_sorted = alloc("w1s_sorted", [P, X_PASSES, HIDDEN], U8)
+        b1_rows = alloc("b1_rows", [P, P], BF16)
+        b1_cols = alloc("b1_cols", [P, 8], F32)
+        b2_all = alloc("b2_all", [P, CODES], BF16)
+        ident32 = alloc("ident32", [P, P], F32)
+        ident16 = alloc("ident16", [P, P], BF16)
+        warm = alloc("warm", [P, 16], F32)
+        zeros = alloc("zeros", [P, PASS], BF16)
+        wide = [alloc("wide%d" % s, [P, TILES, PASS], BF16) for s in range(WIDE_SLOTS)]
+        woven = [alloc("woven%d" % s, [P, 4 * PASS], BF16) for s in range(WOVEN_SLOTS)]
+        codes = {u: alloc("codes_%s%d%d" % u, [P, PASS], U32) for u in units}
+        scales = {u: alloc("scales_%s%d%d" % u, [P, PASS], U8) for u in units}
+        groups = [(half, g) for half in range(2) for g in range(H_PASSES)]
+        h_planes = {k: alloc("h_planes%d%d" % k, [P, 4, PASS], BF16) for k in groups}
+        h_woven = {k: alloc("h_woven%d%d" % k, [P, 4 * PASS], BF16) for k in groups}
+        h_codes = {k: alloc("h_codes%d%d" % k, [P, PASS], U32) for k in groups}
+        h_scales = {k: alloc("h_scales%d%d" % k, [P, PASS], U8) for k in groups}
+        result = [alloc("result%d" % s, [P, PASS], F32) for s in range(RESULT_SLOTS)]
+
+        x_rows = x_bytes.rearrange("(p a) k -> p a k", a=2 * TILES)
+        out_rows = out.rearrange("(p a) n -> p a n", a=2 * TILES)
+
+        def copy_on(engine, dst, src):
+            if engine == "vector":
+                nc.vector.tensor_copy(out=dst, in_=src)
+            else:
+                nc.scalar.copy(out=dst, in_=src)
+
+        def run_step(step):
+            kind = step[0]
+            engine = engine_of[step]
+            if kind == "load_x":
+                half, c = step[1], step[2]
+                nc.sync.dma_start(out=x_raw[(half, c)][:], in_=x_rows[:, TILES * half : TILES * (half + 1), c[0] * PASS : c[1] * PASS])
+            elif kind == "load_x_scale":
+                nc.sync.dma_start(out=x_sc[:], in_=x_scale.rearrange("(p a) j -> p (a j)", a=2 * TILES))
+            elif kind == "load_w2":
+                n = step[1]
+                nc.sync.dma_start(out=w2_raw[n][:], in_=w2_bytes.rearrange("(i p) k -> p i k", p=P)[:, TILES * n : TILES * (n + 1), :])
+            elif kind == "load_w2_scale":
+                nc.sync.dma_start(out=w2_sc[:], in_=w2_scale.rearrange("i j -> (i j)").partition_broadcast(P))
+            elif kind == "load_b2":
+                nc.sync.dma_start(out=b2_all[:], in_=b2.partition_broadcast(P))
+            elif kind == "load_w1":
+                c = step[1]
+                nc.sync.dma_start(out=w1_raw[c][:].bitcast(I32), in_=w1_words[c[0] : c[1]].rearrange("g p b -> p g b").bitcast(I32))
+            elif kind == "fill_w1_scales":
+                nc.vector.memset(w1s_raw[:].bitcast(I32), 0)
+            elif kind == "load_w1_scales":
+                for q in range(4):
+                    nc.sync.dma_start(
+                        out=w1s_raw[32 * q : 32 * q + 4].bitcast(I32),
+                        in_=w1_scales[:, 4 * q : 4 * q + 4, :].rearrange("g r n -> r g n").bitcast(I32),
+                    )
+            elif kind == "fill_b1":
+                nc.vector.memset(b1_rows[:], 0.0)
+            elif kind == "load_b1":
+                for g in range(H_PASSES):
+                    nc.sync.dma_start(
+                        out=b1_rows[4 * g : 4 * g + 4, :].rearrange("t (s w) -> t s w", w=4),
+                        in_=b1[g * PASS : (g + 1) * PASS].rearrange("(s t w) -> t s w", t=4, w=4),
+                    )
+            elif kind == "identities":
+                make_identity(nc, ident32[:])
+                make_identity(nc, ident16[:])
+            elif kind == "fill_warm":
+                nc.vector.memset(warm[:, 0:8], 0.0)
+            elif kind == "fill_zeros":
+                nc.gpsimd.memset(zeros[:].bitcast(I32), 0)
+            elif kind == "warm_tensor":
+                nc.tensor.matmul(banks[bank_of[step]][:], lhsT=zeros[:, 0:P], rhs=zeros[:], start=True, stop=True)
+            elif kind == "warm_scalar":
+                nc.scalar.activation(out=warm[:, 8:16], in_=warm[:, 0:8], func=ACT.Tanh)
+            elif kind == "turn_b1":
+                nc.tensor.transpose(banks[bank_of[("empty_b1",)]][:].bitcast(BF16)[:, 0:P], b1_rows[:], ident16[:])
+            elif kind == "empty_b1":
+                nc.vector.tensor_copy(out=b1_cols[:], in_=banks[bank_of[step]][:].bitcast(BF16)[:, 0:8])
+            elif kind == "sort_words":
+                c, fg = step[1], step[2]
+                src = w1_raw[c][:].bitcast(I32)[:, :, 256 * fg : 256 * (fg + 1)]
+                dst = w1_sorted[:, c[0] : c[1], :].bitcast(I32)[:, :, 256 * fg : 256 * (fg + 1)]
+                nc.vector.tensor_copy(out=dst.rearrange("p g (t s w) -> p g t s w", t=4, w=2), in_=src.rearrange("p g (s t w) -> p g t s w", t=4, w=2))
+            elif kind == "sort_scales":
+                fg = step[1]
+                src = w1s_raw[:].bitcast(I32)[:, :, 128 * fg : 128 * (fg + 1)]
+                dst = w1s_sorted[:].bitcast(I32)[:, :, 128 * fg : 128 * (fg + 1)]
+                nc.vector.tensor_copy(out=dst.rearrange("p g (t s) -> p g t s", t=4), in_=src.rearrange("p g (s t) -> p g t s", t=4))
+            elif kind == "widen":
+                unit, a = step[1], step[2]
+                dst = wide[units.index(unit) % WIDE_SLOTS][:, a, :]
+                for j in range(4):
+                    if unit[0] == "x":
+                        half, g = unit[1], unit[2]
+                        c = chunk_of(X_CHUNKS[half], g)
+                        k0 = (g - c[0]) * PASS + j * P
+                        src = x_raw[(half, c)][:, a, k0 : k0 + P].bitcast(FP8)
+                        col = (TILES * half + a) * (ITEMS // P) + 4 * g + j
+                        scale = x_sc[:, col : col + 1]
+                        if engine == "scalar":
+                            nc.scalar.activation(out=dst[:, j * P : (j + 1) * P], in_=src, func=ACT.Copy, scale=scale)
+                        else:
+                            nc.vector.tensor_scalar(
+                                out=dst.rearrange("p (u m e) -> p m u e", u=2, e=2)[:, 32 * j : 32 * (j + 1)],
+                                in0=src.rearrange("p (m u e) -> p m u e", u=2, e=2),
+                                scalar1=scale, scalar2=None, op0=ALU.mult,
+                            )
+                    else:
+                        n, g = unit[1], unit[2]
+                        src = w2_raw[n][:, a, g * PASS + j * P : g * PASS + (j + 1) * P].bitcast(FP8)
+                        col = (TILES * n + a) * (HIDDEN // P) + 4 * g + j
+                        nc.vector.tensor_scalar(
+                            out=dst[:, j * P : (j + 1) * P].rearrange("p (s w t) -> p s t w", w=4, t=4),
+                            in0=src.rearrange("p (s t w) -> p s t w", t=4, w=4),
+                            scalar1=w2_sc[:, col : col + 1], scalar2=None, op0=ALU.mult,
+                        )
+            elif kind == "turn":
+                unit, pair = step[1], step[2]
+                bank = banks[bank_of[("empty", unit, pair)]]
+                for i in range(2):
+                    a = 2 * pair + i
+                    words = wide[units.index(unit) % WIDE_SLOTS][:, a, :].bitcast(F32)
+                    planar = unit[0] == "x" and engine_of[("widen", unit, a)] == "vector"
+                    for u in range(2):
+                        src = words[:, u * P : (u + 1) * P] if planar else words[:, u : 2 * P : 2]
+                        nc.tensor.transpose(bank[:, (2 * i + u) * P : (2 * i + u + 1) * P], src, ident32[:])
+            elif kind == "empty":
+                unit, pair = step[1], step[2]
+                dst = woven[units.index(unit) % WOVEN_SLOTS][:].bitcast(F32)[:, pair * PASS : (pair + 1) * PASS]
+                copy_on(engine, dst.rearrange("p (i r u) -> p i r u", i=2, u=2), banks[bank_of[step]][:].rearrange("p (i u r) -> p i r u", i=2, u=2))
+            elif kind == "quant":
+                unit = step[1]
+                nc.vector.quantize_mx(out=codes[unit][:].bitcast(FP8X4), scales=scales[unit][:], in_=woven[units.index(unit) % WOVEN_SLOTS][:])
+            elif kind == "mm1":
+                half, f, g = step[1:4]
+                nc.tensor.matmul_mx(
+                    out=banks[bank_of[("relu", half, f)]][:],
+                    lhsT=w1_sorted[:, g, 2 * P * f : 2 * P * (f + 1)].bitcast(FP4X4),
+                    lhsT_scale=w1s_sorted[:, g, P * f : P * (f + 1)],
+                    rhs=codes[("x", half, g)][:].bitcast(FP8X4),
+                    rhs_scale=scales[("x", half, g)][:],
+                    start=(g == 0), stop=(g == X_PASSES - 1),
+                )
+            elif kind == "relu":
+                half, f = step[1], step[2]
+                dst = h_planes[(half, f // 4)][:, f % 4, :]
+                if engine == "scalar":
+                    nc.scalar.activation(out=dst, in_=banks[bank_of[step]][:], func=ACT.Relu, bias=b1_cols[:, f : f + 1])
+                else:
+                    nc.vector.tensor_scalar(out=dst, in0=banks[bank_of[step]][:], scalar1=b1_cols[:, f : f + 1], scalar2=0.0, op0=ALU.add, op1=ALU.max)
+            elif kind == "h_weave":
+                half, g, part = step[1:4]
+                src = h_planes[(half, g)][:, :, part[0] * P : part[1] * P]
+                dst = h_woven[(half, g)][:, 4 * part[0] * P : 4 * part[1] * P]
+                copy_on(engine, dst.rearrange("p (c i t) -> p c t i", i=4, t=4), src.rearrange("p t (c i) -> p c t i", i=4))
+            elif kind == "h_quant":
+                half, g, part = step[1:4]
+                cols = slice(part[0] * P, part[1] * P)
+                nc.vector.quantize_mx(
+                    out=h_codes[(half, g)][:, cols].bitcast(FP8X4),
+                    scales=h_scales[(half, g)][:, cols],
+                    in_=h_woven[(half, g)][:, 4 * part[0] * P : 4 * part[1] * P],
+                )
+            elif kind == "mm2":
+                (half, a, n), g = step[1], step[2]
+                nc.tensor.matmul_mx(
+                    out=banks[bank_of[("bias", step[1])]][:],
+                    lhsT=h_codes[(half, g)][:, a * P : (a + 1) * P].bitcast(FP8X4),
+                    lhsT_scale=h_scales[(half, g)][:, a * P : (a + 1) * P],
+                    rhs=codes[("w", n, g)][:].bitcast(FP8X4),
+                    rhs_scale=scales[("w", n, g)][:],
+                    start=(g == 0), stop=(g == H_PASSES - 1),
+                )
+            elif kind == "bias":
+                n = step[1][2]
+                nc.vector.tensor_tensor(
+                    out=result[results.index(step[1]) % RESULT_SLOTS][:], in0=banks[bank_of[step]][:],
+                    in1=b2_all[:, n * PASS : (n + 1) * PASS], op=ALU.add,
+                )
+            elif kind == "tanh":
+                tile = result[results.index(step[1]) % RESULT_SLOTS]
+                nc.scalar.activation(out=tile[:], in_=tile[:], func=ACT.Tanh)
+            else:
+                half, a, n = step[1]
+                nc.sync.dma_start(
+                    out=out_rows[:, TILES * half + a, n * PASS : (n + 1) * PASS],
+                    in_=result[results.index(step[1]) % RESULT_SLOTS][:],
+                )
+
+        done = set()
+        position = {engine: 0 for engine in orders}
+        with tc.manual_schedule():
+            while any(position[engine] < len(order) for engine, order in orders.items()):
+                progress = False
+                for engine, order in orders.items():
+                    while position[engine] < len(order) and all(s in done for s in needs[order[position[engine]]]):
+                        step = order[position[engine]]
+                        run_step(step)
+                        done.add(step)
+                        position[engine] += 1
+                        progress = True
+                assert progress

@@ -24,9 +24,10 @@ H_PASSES = HIDDEN // PASS
 TILES = 4
 X_CHUNKS = [[(0, 1), (1, 2), (2, 4), (4, 6)], [(0, 2), (2, 4), (4, 6)]]
 W1_CHUNKS = [(0, 1), (1, 2), (2, 4), (4, 6)]
-WIDE_SLOTS = 8
+SCALE_CHUNKS = [(0, 2), (2, 6)]
+WIDE_SLOTS = 6
 WOVEN_SLOTS = 4
-RESULT_SLOTS = 8
+RESULT_SLOTS = 10
 
 
 def chunk_of(chunks, g):
@@ -38,6 +39,8 @@ def engine_orders():
     xb = [("x", 1, g) for g in range(X_PASSES)]
     w2 = [("w", n, g) for n in range(2) for g in range(H_PASSES)]
     stream = xa + xb + w2
+    whole = (0, TILES)
+    single = [(a, a + 1) for a in range(TILES)]
     bank_of = {}
     tensor = []
 
@@ -46,8 +49,8 @@ def engine_orders():
             bank_of[("empty", unit, pair)] = first_bank + pair
             tensor.append(("turn", unit, pair))
 
-    def mm1(half, fs, gs):
-        tensor.extend(("mm1", half, f, g) for g in gs for f in fs)
+    def mm1(half, fs, gs, part=whole):
+        tensor.extend(("mm1", half, f, part, g) for g in gs for f in fs)
 
     def mm2(key, bank, gs):
         bank_of[("bias", key)] = bank
@@ -59,9 +62,11 @@ def engine_orders():
             tensor.append(("warm_tensor", i))
 
     for f, bank in enumerate([0, 1, 2, 3, 4, 5, 0, 1]):
-        bank_of[("relu", 0, f)] = bank
-    for f, bank in enumerate([2, 3, 4, 5, 6, 2, 4, 6]):
-        bank_of[("relu", 1, f)] = bank
+        bank_of[("relu", 0, f, whole)] = bank
+    for f, bank in enumerate([2, 3, 4, 5, 6, 7, 4]):
+        bank_of[("relu", 1, f, whole)] = bank
+    for part, bank in zip(single, [2, 3, 6, 5]):
+        bank_of[("relu", 1, 7, part)] = bank
     bank_of[("empty_b1",)] = 0
     warm(0, 6)
     tensor.append(("turn_b1",))
@@ -80,33 +85,25 @@ def engine_orders():
     turn(xb[4], 0)
     mm1(1, range(4), [1, 2])
     turn(xb[5], 6)
-    turn(w2[0], 0)
-    mm1(1, range(4), [3, 4])
-    turn(w2[1], 6)
-    turn(w2[2], 0)
-    mm1(1, range(4), [5])
+    mm1(1, range(4), [3, 4, 5])
     keys_a = [(0, a, n) for n in range(2) for a in range(TILES)]
     keys_b = [(1, a, n) for a in range(TILES) for n in range(2)]
     mm1(1, [4], range(X_PASSES))
-    turn(w2[3], 0)
-    mm2(keys_a[0], 7, range(2))
-    mm2(keys_a[1], 3, range(2))
+    turn(w2[0], 0)
+    turn(w2[1], 2)
     mm1(1, [5], range(X_PASSES))
-    mm2(keys_a[2], 5, range(2))
-    mm2(keys_a[3], 7, range(2))
+    turn(w2[2], 4)
+    turn(w2[3], 0)
+    for key, bank in zip(keys_a[:4], [2, 3, 6, 5]):
+        mm2(key, bank, range(2))
     mm1(1, [6], range(X_PASSES))
-    mm2(keys_a[4], 0, range(2))
-    mm2(keys_a[5], 1, range(2))
-    mm1(1, [7], range(X_PASSES))
-    mm2(keys_a[6], 3, range(2))
-    mm2(keys_a[7], 5, range(2))
-    tail_banks = [7, 2, 0, 1, 4, 6, 3, 5]
-    for i, key in enumerate(keys_b[:4]):
-        mm2(key, tail_banks[i], [0])
-    for i, key in enumerate(keys_b[:4]):
-        mm2(key, tail_banks[i], [1])
-    for i, key in enumerate(keys_b[4:]):
-        mm2(key, tail_banks[4 + i], range(2))
+    for key, bank in zip(keys_a[4:7], [7, 0, 1]):
+        mm2(key, bank, range(2))
+    for part in single:
+        mm1(1, [7], range(X_PASSES), part)
+    mm2(keys_a[7], 4, range(2))
+    for key, bank in zip(keys_b, [7, 0, 1, 2, 3, 6, 5, 4]):
+        mm2(key, bank, range(2))
 
     def widen(unit, tiles):
         return [("widen", unit, a) for a in tiles]
@@ -114,7 +111,13 @@ def engine_orders():
     def empty(unit):
         return [("empty", unit, 0), ("empty", unit, 1)]
 
-    helped = [0, 1, 2, 3]
+    def split(unit):
+        return [("split", unit, 0), ("split", unit, 1)]
+
+    def relu(half, fs):
+        return [("relu", half, f, whole) for f in fs]
+
+    helped = [0, 1, 2, 3, 4, 5, 6, 7, 8]
 
     def own(i):
         return widen(stream[i], range(3) if i in helped else range(4))
@@ -122,35 +125,37 @@ def engine_orders():
     def aid(i):
         return widen(stream[i], [3]) if i in helped else []
 
-    whole = (0, TILES)
-    vector = [("fill_warm",), ("fill_b1",), ("fill_w1_scales",)]
-    vector += own(0) + [("empty_b1",), ("sort_words", W1_CHUNKS[0], 0)] + own(1) + [("sort_scales", 0), ("quant", xa[0])]
-    vector += [("sort_scales", 1), ("sort_words", W1_CHUNKS[0], 1)] + own(2)[:1] + [("quant", xa[1])] + own(2)[1:]
-    vector += [("sort_words", W1_CHUNKS[1], 0), ("sort_words", W1_CHUNKS[1], 1)]
-    vector += own(3) + [("sort_words", W1_CHUNKS[2], 0), ("quant", xa[2]), ("sort_words", W1_CHUNKS[2], 1)]
-    vector += own(4) + [("quant", xa[3])] + own(5) + [("sort_words", W1_CHUNKS[3], 0), ("quant", xa[4]), ("sort_words", W1_CHUNKS[3], 1)]
-    vector += own(6) + [("quant", xa[5])] + own(7) + own(8) + [("quant", xb[0])] + own(9) + own(10) + [("quant", xb[1])]
-    vector += own(11) + own(12) + [("quant", xb[2])] + own(13) + [("quant", xb[3]), ("h_weave", 0, 0, whole), ("quant", xb[4])]
-    vector += own(14) + [("quant", xb[5])] + own(15) + [("quant", w2[0]), ("h_quant", 0, 0, whole), ("h_quant", 0, 1, whole), ("quant", w2[1]), ("quant", w2[2])]
-    vector += [("h_weave", 1, 0, whole), ("quant", w2[3])] + [("bias", key) for key in keys_a[:2]] + [("h_quant", 1, 0, whole)]
-    vector += [("bias", key) for key in keys_a[2:6]]
-    vector += [("h_weave", 1, 1, (0, 1)), ("h_weave", 1, 1, (1, 2)), ("h_quant", 1, 1, (0, 1)), ("h_weave", 1, 1, (2, 3)), ("h_quant", 1, 1, (1, 2)), ("bias", keys_a[6]), ("h_quant", 1, 1, (2, 4)), ("bias", keys_a[7])]
-    vector += [("bias", key) for key in keys_b]
+    def sort(i):
+        return [("sort_words", W1_CHUNKS[i]), ("sort_scales", W1_CHUNKS[i])]
 
-    scalar = [("warm_scalar",)] + aid(0) + [("empty", xa[0], 0)] + aid(1) + [("empty", xa[0], 1)] + empty(xa[1]) + aid(2)
-    for i in range(2, 8):
-        scalar += aid(i + 1) + empty(stream[i]) if i < 7 else []
-    scalar += [("relu", 0, 0), ("relu", 0, 1)] + empty(xb[1]) + [("relu", 0, f) for f in range(2, 5)] + empty(xb[2]) + [("relu", 0, f) for f in range(5, 8)] + empty(xb[3]) + empty(xb[4])
-    scalar += [("h_weave", 0, 1, (0, 2))] + empty(xb[5]) + empty(w2[0]) + [("h_weave", 0, 1, (2, 4))] + empty(w2[1]) + empty(w2[2])
-    scalar += [("relu", 1, f) for f in range(4)] + empty(w2[3])
-    scalar += [("relu", 1, 4)] + [("tanh", key) for key in keys_a[:2]] + [("relu", 1, 5), ("tanh", keys_a[2]), ("tanh", keys_a[3]), ("relu", 1, 6), ("tanh", keys_a[4]), ("tanh", keys_a[5]), ("relu", 1, 7), ("h_weave", 1, 1, (3, 4))]
-    scalar += [("tanh", key) for key in keys_a[6:] + keys_b]
+    vector = [("fill_zeros",), ("fill_w1_scales",), ("fill_warm",), ("fill_b1",), ("unit_column",), ("sort_b1",)]
+    vector += own(0) + [("empty_b1",)] + sort(0)[:1] + own(1) + sort(0)[1:] + [("quant", xa[0])]
+    vector += sort(1) + own(2)[:1] + [("quant", xa[1])] + own(2)[1:]
+    vector += own(3) + sort(2)[:1] + [("quant", xa[2])] + sort(2)[1:]
+    vector += own(4) + own(5)[:1] + [("quant", xa[3])] + own(5)[1:] + sort(3) + [("quant", xa[4])]
+    vector += own(6) + own(7)[:1] + [("quant", xa[5])] + own(7)[1:] + own(8) + [("quant", xb[0])] + own(9) + [("quant", xb[1])] + own(10)
+    vector += own(11) + [("quant", xb[2])] + own(12) + [("h_weave", 0, 0, whole), ("quant", xb[3])] + own(13)[:2] + [("quant", xb[4])] + own(13)[2:] + split(w2[0])
+    vector += [("quant", xb[5])] + split(w2[1]) + own(14) + own(15) + [("h_quant", 0, 0, whole)] + split(w2[3]) + [("h_quant", 0, 1, whole), ("quant", w2[0])]
+    vector += [("h_weave", 1, 0, (0, 2)), ("quant", w2[1]), ("h_weave", 1, 0, (2, 4)), ("quant", w2[2]), ("bias", keys_a[0]), ("bias", keys_a[1]), ("quant", w2[3]), ("bias", keys_a[2]), ("bias", keys_a[3]), ("h_quant", 1, 0, whole)]
+    vector += [("bias", key) for key in keys_a[4:7]]
+    vector += [("h_weave", 1, 1, single[0]), ("h_weave", 1, 1, single[1]), ("h_quant", 1, 1, single[0]), ("h_weave", 1, 1, single[2]), ("h_quant", 1, 1, single[1]), ("bias", keys_a[7])]
+    vector += [("h_quant", 1, 1, single[2]), ("bias", keys_b[0]), ("h_quant", 1, 1, single[3])]
+    vector += [("bias", key) for key in keys_b[1:]]
 
-    sync = [("load_x_scale",), ("load_x", 0, X_CHUNKS[0][0]), ("load_b1",), ("load_w1", W1_CHUNKS[0]), ("load_x", 0, X_CHUNKS[0][1]), ("load_w1_scales",)]
-    sync += [("load_x", 0, X_CHUNKS[0][2]), ("load_w1", W1_CHUNKS[1]), ("load_w1", W1_CHUNKS[2]), ("load_x", 0, X_CHUNKS[0][3]), ("load_w1", W1_CHUNKS[3])]
+    scalar = [("warm_scalar",)] + aid(0) + empty(xa[0]) + aid(1) + empty(xa[1]) + aid(2)
+    scalar += aid(3) + empty(xa[2]) + aid(4) + aid(5) + empty(xa[3]) + aid(6) + aid(7) + empty(xa[4]) + aid(8) + empty(xa[5]) + aid(9) + empty(xb[0])
+    scalar += relu(0, [0, 1]) + empty(xb[1]) + relu(0, [2, 3, 4]) + empty(xb[2]) + relu(0, [5, 6, 7]) + empty(xb[3]) + empty(xb[4])
+    scalar += [("h_weave", 0, 1, (0, 2))] + empty(xb[5]) + [("h_weave", 0, 1, (2, 4))]
+    scalar += relu(1, [0, 1, 2, 3]) + split(w2[2])[:1] + empty(w2[0]) + split(w2[2])[1:] + empty(w2[1]) + relu(1, [4]) + empty(w2[2]) + empty(w2[3]) + relu(1, [5])
+    scalar += [("tanh", key) for key in keys_a[0:3]] + relu(1, [6]) + [("tanh", key) for key in keys_a[3:5]]
+    scalar += [("relu", 1, 7, single[0]), ("tanh", keys_a[5]), ("relu", 1, 7, single[1]), ("relu", 1, 7, single[2]), ("tanh", keys_a[6]), ("relu", 1, 7, single[3]), ("h_weave", 1, 1, single[3])]
+    scalar += [("tanh", key) for key in keys_a[7:] + keys_b]
+
+    sync = [("load_b1",), ("load_x_scale",), ("load_x", 0, X_CHUNKS[0][0]), ("load_w1", W1_CHUNKS[0]), ("load_x", 0, X_CHUNKS[0][1]), ("load_w1_scales", SCALE_CHUNKS[0])]
+    sync += [("load_w1", W1_CHUNKS[1]), ("load_x", 0, X_CHUNKS[0][2]), ("load_w1_scales", SCALE_CHUNKS[1]), ("load_w1", W1_CHUNKS[2]), ("load_x", 0, X_CHUNKS[0][3]), ("load_w1", W1_CHUNKS[3])]
     sync += [("load_x", 1, c) for c in X_CHUNKS[1]] + [("load_w2_scale",), ("load_w2", 0), ("load_w2", 1), ("load_b2",)]
     sync += [("store", key) for key in keys_a + keys_b]
-    return {"sync": sync, "gpsimd": [("fill_zeros",), ("identities",)], "vector": vector, "scalar": scalar, "tensor": tensor}, bank_of
+    return {"sync": sync, "gpsimd": [("identities",)], "vector": vector, "scalar": scalar, "tensor": tensor}, bank_of
 
 
 def prerequisites(orders):
@@ -173,8 +178,12 @@ def prerequisites(orders):
                 before += [("load_w2", unit[1]), ("load_w2_scale",)]
             if units.index(unit) >= WIDE_SLOTS:
                 before.append(("turn", units[units.index(unit) - WIDE_SLOTS], a // 2))
+        elif kind == "split":
+            before += [("widen", step[1], 2 * step[2]), ("widen", step[1], 2 * step[2] + 1)]
         elif kind == "turn":
             before += [("widen", step[1], 2 * step[2]), ("widen", step[1], 2 * step[2] + 1), ("identities",)]
+            if ("split",) + step[1:] in steps:
+                before.append(("split",) + step[1:])
         elif kind == "empty":
             before.append(("turn", step[1], step[2]))
             if units.index(step[1]) >= WOVEN_SLOTS:
@@ -187,23 +196,25 @@ def prerequisites(orders):
             before.append(("fill_zeros",))
         elif kind == "warm_scalar":
             before.append(("fill_warm",))
-        elif kind == "load_b1":
-            before.append(("fill_b1",))
+        elif kind == "sort_b1":
+            before += [("fill_b1",), ("load_b1",)]
+        elif kind == "unit_column":
+            before.append(("identities",))
         elif kind == "sort_words":
             before.append(("load_w1", step[1]))
         elif kind == "sort_scales":
-            before.append(("load_w1_scales",))
+            before.append(("load_w1_scales", chunk_of(SCALE_CHUNKS, step[1][0])))
         elif kind == "turn_b1":
-            before += [("load_b1",), ("identities",)]
+            before += [("sort_b1",), ("unit_column",)]
         elif kind == "empty_b1":
             before.append(("turn_b1",))
         elif kind == "mm1":
-            half, f, g = step[1:4]
-            before += [("quant", ("x", half, g)), ("sort_words", chunk_of(W1_CHUNKS, g), f // 4), ("sort_scales", f // 4)]
+            half, f, part, g = step[1:5]
+            before += [("quant", ("x", half, g)), ("sort_words", chunk_of(W1_CHUNKS, g)), ("sort_scales", chunk_of(W1_CHUNKS, g))]
         elif kind == "relu":
-            before += [("mm1", step[1], step[2], X_PASSES - 1), ("empty_b1",)]
+            before += [("mm1",) + step[1:] + (X_PASSES - 1,), ("empty_b1",)]
         elif kind == "h_weave":
-            before += [("relu", step[1], 4 * step[2] + t) for t in range(4)]
+            before += [s for s in steps if s[:2] == ("relu", step[1]) and s[2] // 4 == step[2] and s[3][0] < step[3][1] and step[3][0] < s[3][1]]
         elif kind == "h_quant":
             before += [s for s in steps if s[:3] == ("h_weave",) + step[1:3] and s[3][0] < step[3][1] and step[3][0] < s[3][1]]
         elif kind == "mm2":
@@ -232,7 +243,7 @@ def tile_click_autoencoder_encoder_d6_kernel(
 
     emptied_by = {}
     for step in orders["tensor"]:
-        tenant = {"turn": ("empty",) + step[1:], "turn_b1": ("empty_b1",), "mm1": ("relu",) + step[1:3], "mm2": ("bias",) + step[1:2]}.get(step[0])
+        tenant = {"turn": ("empty",) + step[1:], "turn_b1": ("empty_b1",), "mm1": ("relu",) + step[1:4], "mm2": ("bias",) + step[1:2]}.get(step[0])
         if tenant is None:
             continue
         bank = bank_of[tenant]
@@ -260,14 +271,16 @@ def tile_click_autoencoder_encoder_d6_kernel(
         w1_sorted = alloc("w1_sorted", [P, X_PASSES, 2 * HIDDEN], U8)
         w1s_raw = alloc("w1s_raw", [P, X_PASSES, HIDDEN], U8)
         w1s_sorted = alloc("w1s_sorted", [P, X_PASSES, HIDDEN], U8)
-        b1_rows = alloc("b1_rows", [P, P], BF16)
+        b1_raw = alloc("b1_raw", [1, HIDDEN], BF16)
+        b1_rows = alloc("b1_rows", [P, HIDDEN], BF16)
         b1_cols = alloc("b1_cols", [P, 8], F32)
         b2_all = alloc("b2_all", [P, CODES], BF16)
         ident32 = alloc("ident32", [P, P], F32)
-        ident16 = alloc("ident16", [P, P], BF16)
+        unit_col = alloc("unit_col", [P, 2], BF16)
         warm = alloc("warm", [P, 16], F32)
         zeros = alloc("zeros", [P, PASS], BF16)
         wide = [alloc("wide%d" % s, [P, TILES, PASS], BF16) for s in range(WIDE_SLOTS)]
+        w2_split = {s[1]: alloc("w2_split%d%d" % s[1][1:], [P, TILES, PASS], BF16) for s in engine_of if s[0] == "split" and s[2] == 0}
         woven = [alloc("woven%d" % s, [P, 4 * PASS], BF16) for s in range(WOVEN_SLOTS)]
         codes = {u: alloc("codes_%s%d%d" % u, [P, PASS], U32) for u in units}
         scales = {u: alloc("scales_%s%d%d" % u, [P, PASS], U8) for u in units}
@@ -308,44 +321,48 @@ def tile_click_autoencoder_encoder_d6_kernel(
             elif kind == "fill_w1_scales":
                 nc.vector.memset(w1s_raw[:].bitcast(I32), 0)
             elif kind == "load_w1_scales":
+                c = step[1]
                 for q in range(4):
                     nc.sync.dma_start(
-                        out=w1s_raw[32 * q : 32 * q + 4].bitcast(I32),
-                        in_=w1_scales[:, 4 * q : 4 * q + 4, :].rearrange("g r n -> r g n").bitcast(I32),
+                        out=w1s_raw[32 * q : 32 * q + 4, c[0] : c[1], :].bitcast(I32),
+                        in_=w1_scales[c[0] : c[1], 4 * q : 4 * q + 4, :].rearrange("g r n -> r g n").bitcast(I32),
                     )
             elif kind == "fill_b1":
-                nc.vector.memset(b1_rows[:], 0.0)
+                nc.vector.memset(b1_rows[:].bitcast(I32), 0)
             elif kind == "load_b1":
-                for g in range(H_PASSES):
-                    nc.sync.dma_start(
-                        out=b1_rows[4 * g : 4 * g + 4, :].rearrange("t (s w) -> t s w", w=4),
-                        in_=b1[g * PASS : (g + 1) * PASS].rearrange("(s t w) -> t s w", t=4, w=4),
-                    )
+                nc.sync.dma_start(out=b1_raw[:], in_=b1.rearrange("(o f) -> o f", o=1))
+            elif kind == "sort_b1":
+                nc.vector.tensor_copy(
+                    out=b1_rows[0:1, :].rearrange("o (g t s w) -> o g t s w", g=H_PASSES, t=4, w=4),
+                    in_=b1_raw[:].rearrange("o (g s t w) -> o g t s w", g=H_PASSES, t=4, w=4),
+                )
             elif kind == "identities":
                 make_identity(nc, ident32[:])
-                make_identity(nc, ident16[:])
+            elif kind == "unit_column":
+                nc.vector.tensor_copy(out=unit_col[:], in_=ident32[:, 0:2])
             elif kind == "fill_warm":
                 nc.vector.memset(warm[:, 0:8], 0.0)
             elif kind == "fill_zeros":
-                nc.gpsimd.memset(zeros[:].bitcast(I32), 0)
+                nc.vector.memset(zeros[:].bitcast(I32), 0)
             elif kind == "warm_tensor":
                 nc.tensor.matmul(banks[bank_of[step]][:], lhsT=zeros[:, 0:P], rhs=zeros[:], start=True, stop=True)
             elif kind == "warm_scalar":
                 nc.scalar.activation(out=warm[:, 8:16], in_=warm[:, 0:8], func=ACT.Tanh)
             elif kind == "turn_b1":
-                nc.tensor.transpose(banks[bank_of[("empty_b1",)]][:].bitcast(BF16)[:, 0:P], b1_rows[:], ident16[:])
+                for f in range(8):
+                    nc.tensor.matmul(banks[bank_of[("empty_b1",)]][:, 2 * f : 2 * f + 2], lhsT=b1_rows[:, f * P : (f + 1) * P], rhs=unit_col[:], start=True, stop=True)
             elif kind == "empty_b1":
-                nc.vector.tensor_copy(out=b1_cols[:], in_=banks[bank_of[step]][:].bitcast(BF16)[:, 0:8])
+                nc.vector.tensor_copy(out=b1_cols[:], in_=banks[bank_of[step]][:, 0:16:2])
             elif kind == "sort_words":
-                c, fg = step[1], step[2]
-                src = w1_raw[c][:].bitcast(I32)[:, :, 256 * fg : 256 * (fg + 1)]
-                dst = w1_sorted[:, c[0] : c[1], :].bitcast(I32)[:, :, 256 * fg : 256 * (fg + 1)]
-                nc.vector.tensor_copy(out=dst.rearrange("p g (t s w) -> p g t s w", t=4, w=2), in_=src.rearrange("p g (s t w) -> p g t s w", t=4, w=2))
+                c = step[1]
+                src = w1_raw[c][:].bitcast(I32).rearrange("p g (h s t w) -> p (g h) t s w", h=H_PASSES, t=4, w=2)
+                dst = w1_sorted[:, c[0] : c[1], :].bitcast(I32).rearrange("p g (h t s w) -> p (g h) t s w", h=H_PASSES, t=4, w=2)
+                nc.vector.tensor_copy(out=dst, in_=src)
             elif kind == "sort_scales":
-                fg = step[1]
-                src = w1s_raw[:].bitcast(I32)[:, :, 128 * fg : 128 * (fg + 1)]
-                dst = w1s_sorted[:].bitcast(I32)[:, :, 128 * fg : 128 * (fg + 1)]
-                nc.vector.tensor_copy(out=dst.rearrange("p g (t s) -> p g t s", t=4), in_=src.rearrange("p g (s t) -> p g t s", t=4))
+                c = step[1]
+                src = w1s_raw[:, c[0] : c[1], :].bitcast(I32).rearrange("p g (h s t) -> p (g h) t s", h=H_PASSES, t=4)
+                dst = w1s_sorted[:, c[0] : c[1], :].bitcast(I32).rearrange("p g (h t s) -> p (g h) t s", h=H_PASSES, t=4)
+                nc.vector.tensor_copy(out=dst, in_=src)
             elif kind == "widen":
                 unit, a = step[1], step[2]
                 dst = wide[units.index(unit) % WIDE_SLOTS][:, a, :]
@@ -374,6 +391,11 @@ def tile_click_autoencoder_encoder_d6_kernel(
                             in0=src.rearrange("p (s t w) -> p s t w", t=4, w=4),
                             scalar1=w2_sc[:, col : col + 1], scalar2=None, op0=ALU.mult,
                         )
+            elif kind == "split":
+                unit, pair = step[1], step[2]
+                src = wide[units.index(unit) % WIDE_SLOTS][:, 2 * pair : 2 * pair + 2, :].bitcast(F32)
+                dst = w2_split[unit][:, 2 * pair : 2 * pair + 2, :].bitcast(F32)
+                copy_on(engine, dst.rearrange("p i (u m) -> p i u m", u=2), src.rearrange("p i (m u) -> p i u m", u=2))
             elif kind == "turn":
                 unit, pair = step[1], step[2]
                 bank = banks[bank_of[("empty", unit, pair)]]
@@ -381,6 +403,8 @@ def tile_click_autoencoder_encoder_d6_kernel(
                     a = 2 * pair + i
                     words = wide[units.index(unit) % WIDE_SLOTS][:, a, :].bitcast(F32)
                     planar = unit[0] == "x" and engine_of[("widen", unit, a)] == "vector"
+                    if ("split", unit, pair) in engine_of:
+                        words, planar = w2_split[unit][:, a, :].bitcast(F32), True
                     for u in range(2):
                         src = words[:, u * P : (u + 1) * P] if planar else words[:, u : 2 * P : 2]
                         nc.tensor.transpose(bank[:, (2 * i + u) * P : (2 * i + u + 1) * P], src, ident32[:])
@@ -392,22 +416,24 @@ def tile_click_autoencoder_encoder_d6_kernel(
                 unit = step[1]
                 nc.vector.quantize_mx(out=codes[unit][:].bitcast(FP8X4), scales=scales[unit][:], in_=woven[units.index(unit) % WOVEN_SLOTS][:])
             elif kind == "mm1":
-                half, f, g = step[1:4]
+                half, f, part, g = step[1:5]
+                cols = slice(part[0] * P, part[1] * P)
                 nc.tensor.matmul_mx(
-                    out=banks[bank_of[("relu", half, f)]][:],
+                    out=banks[bank_of[("relu", half, f, part)]][:, 0 : (part[1] - part[0]) * P],
                     lhsT=w1_sorted[:, g, 2 * P * f : 2 * P * (f + 1)].bitcast(FP4X4),
                     lhsT_scale=w1s_sorted[:, g, P * f : P * (f + 1)],
-                    rhs=codes[("x", half, g)][:].bitcast(FP8X4),
-                    rhs_scale=scales[("x", half, g)][:],
+                    rhs=codes[("x", half, g)][:, cols].bitcast(FP8X4),
+                    rhs_scale=scales[("x", half, g)][:, cols],
                     start=(g == 0), stop=(g == X_PASSES - 1),
                 )
             elif kind == "relu":
-                half, f = step[1], step[2]
-                dst = h_planes[(half, f // 4)][:, f % 4, :]
+                half, f, part = step[1:4]
+                dst = h_planes[(half, f // 4)][:, f % 4, part[0] * P : part[1] * P]
+                src = banks[bank_of[step]][:, 0 : (part[1] - part[0]) * P]
                 if engine == "scalar":
-                    nc.scalar.activation(out=dst, in_=banks[bank_of[step]][:], func=ACT.Relu, bias=b1_cols[:, f : f + 1])
+                    nc.scalar.activation(out=dst, in_=src, func=ACT.Relu, bias=b1_cols[:, f : f + 1])
                 else:
-                    nc.vector.tensor_scalar(out=dst, in0=banks[bank_of[step]][:], scalar1=b1_cols[:, f : f + 1], scalar2=0.0, op0=ALU.add, op1=ALU.max)
+                    nc.vector.tensor_scalar(out=dst, in0=src, scalar1=b1_cols[:, f : f + 1], scalar2=0.0, op0=ALU.add, op1=ALU.max)
             elif kind == "h_weave":
                 half, g, part = step[1:4]
                 src = h_planes[(half, g)][:, :, part[0] * P : part[1] * P]

@@ -117,13 +117,13 @@ def engine_orders():
     def relu(half, fs):
         return [("relu", half, f, whole) for f in fs]
 
-    helped = [0, 1, 2, 3, 4, 5, 6, 7, 8]
+    helped = [1, 1, 1, 1, 1, 1, 1, 1, 2, 2] + [0] * 6
 
     def own(i):
-        return widen(stream[i], range(3) if i in helped else range(4))
+        return widen(stream[i], range(TILES - helped[i]))
 
     def aid(i):
-        return widen(stream[i], [3]) if i in helped else []
+        return widen(stream[i], range(TILES - helped[i], TILES))
 
     def sort(i):
         return [("sort_words", W1_CHUNKS[i]), ("sort_scales", W1_CHUNKS[i])]
@@ -133,9 +133,9 @@ def engine_orders():
     vector += sort(1) + own(2)[:1] + [("quant", xa[1])] + own(2)[1:]
     vector += own(3) + sort(2)[:1] + [("quant", xa[2])] + sort(2)[1:]
     vector += own(4) + own(5)[:1] + [("quant", xa[3])] + own(5)[1:] + sort(3) + [("quant", xa[4])]
-    vector += own(6) + own(7)[:1] + [("quant", xa[5])] + own(7)[1:] + own(8) + [("quant", xb[0])] + own(9) + [("quant", xb[1])] + own(10)
-    vector += own(11) + [("quant", xb[2])] + own(12) + [("h_weave", 0, 0, whole), ("quant", xb[3])] + own(13)[:2] + [("quant", xb[4])] + own(13)[2:] + split(w2[0])
-    vector += [("quant", xb[5])] + split(w2[1]) + own(14) + own(15) + [("h_quant", 0, 0, whole)] + split(w2[3]) + [("h_quant", 0, 1, whole), ("quant", w2[0])]
+    vector += own(6) + own(7)[:2] + [("quant", xa[5])] + own(7)[2:] + own(8) + own(9)[:1] + [("quant", xb[0])] + own(9)[1:] + own(10) + [("quant", xb[1])]
+    vector += own(11) + [("quant", xb[2])] + own(12) + [("h_weave", 0, 0, whole), ("quant", xb[3]), ("quant", xb[4])] + own(13) + split(w2[0])[:1]
+    vector += [("quant", xb[5])] + split(w2[0])[1:] + split(w2[1]) + own(14) + own(15) + [("h_quant", 0, 0, whole)] + split(w2[3]) + [("h_quant", 0, 1, whole), ("quant", w2[0])]
     vector += [("h_weave", 1, 0, (0, 2)), ("quant", w2[1]), ("h_weave", 1, 0, (2, 4)), ("quant", w2[2]), ("bias", keys_a[0]), ("bias", keys_a[1]), ("quant", w2[3]), ("bias", keys_a[2]), ("bias", keys_a[3]), ("h_quant", 1, 0, whole)]
     vector += [("bias", key) for key in keys_a[4:7]]
     vector += [("h_weave", 1, 1, single[0]), ("h_weave", 1, 1, single[1]), ("h_quant", 1, 1, single[0]), ("h_weave", 1, 1, single[2]), ("h_quant", 1, 1, single[1]), ("bias", keys_a[7])]

from contextlib import ExitStack

import concourse.mybir as mybir
from concourse.masks import make_identity

USERS, ITEMS, HIDDEN, CODES = 1024, 3072, 1024, 1024
FLOPS = 2 * USERS * ITEMS * HIDDEN + 2 * USERS * HIDDEN * CODES

F32 = mybir.dt.float32
BF16 = mybir.dt.bfloat16
I32 = mybir.dt.int32
U32 = mybir.dt.uint32
U8 = mybir.dt.uint8
FP8 = mybir.dt.float8_e4m3fn
FP8X4 = mybir.dt.float8_e4m3fn_x4
FP4X4 = mybir.dt.float4_e2m1fn_x4
ACT = mybir.ActivationFunctionType
ALU = mybir.AluOpType

P = 128
PASS = 512
X_PASSES = ITEMS // PASS
H_PASSES = HIDDEN // PASS
TILES = 4
X_CHUNKS = [[(0, 1), (1, 2), (2, 4), (4, 6)], [(0, 2), (2, 4), (4, 6)]]
W1_CHUNKS = [(0, 1), (1, 2), (2, 4), (4, 6)]
SCALE_CHUNKS = [(0, 2), (2, 6)]
WIDE_SLOTS = 6
WOVEN_SLOTS = 4
RESULT_SLOTS = 10


def chunk_of(chunks, g):
    return [c for c in chunks if c[0] <= g < c[1]][0]


def engine_orders():
    xa = [("x", 0, g) for g in range(X_PASSES)]
    xb = [("x", 1, g) for g in range(X_PASSES)]
    w2 = [("w", n, g) for n in range(2) for g in range(H_PASSES)]
    stream = xa + xb + w2
    whole = (0, TILES)
    single = [(a, a + 1) for a in range(TILES)]
    bank_of = {}
    tensor = []

    def turn(unit, first_bank):
        for pair in range(2):
            bank_of[("empty", unit, pair)] = first_bank + pair
            tensor.append(("turn", unit, pair))

    def mm1(half, fs, gs, part=whole):
        tensor.extend(("mm1", half, f, part, g) for g in gs for f in fs)

    def mm2(key, bank, gs):
        bank_of[("bias", key)] = bank
        tensor.extend(("mm2", key, g) for g in gs)

    def warm(first, count):
        for i in range(first, first + count):
            bank_of[("warm_tensor", i)] = 1
            tensor.append(("warm_tensor", i))

    for f, bank in enumerate([0, 1, 2, 3, 4, 5, 0, 1]):
        bank_of[("relu", 0, f, whole)] = bank
    for f, bank in enumerate([2, 3, 4, 5, 6, 7, 4]):
        bank_of[("relu", 1, f, whole)] = bank
    for part, bank in zip(single, [2, 3, 6, 5]):
        bank_of[("relu", 1, 7, part)] = bank
    bank_of[("empty_b1",)] = 0
    warm(0, 6)
    tensor.append(("turn_b1",))
    turn(xa[0], 6)
    warm(10, 2)
    turn(xa[1], 4)
    warm(20, 1)
    for g in range(X_PASSES):
        mm1(0, range(6), [g])
        turn(stream[g + 2], 6)
    mm1(0, [6], range(X_PASSES))
    turn(xb[2], 6)
    mm1(0, [7], range(X_PASSES))
    mm1(1, range(4), [0])
    turn(xb[3], 6)
    turn(xb[4], 0)
    mm1(1, range(4), [1, 2])
    turn(xb[5], 6)
    mm1(1, range(4), [3, 4, 5])
    keys_a = [(0, a, n) for n in range(2) for a in range(TILES)]
    keys_b = [(1, a, n) for a in range(TILES) for n in range(2)]
    mm1(1, [4], range(X_PASSES))
    turn(w2[0], 0)
    turn(w2[1], 2)
    mm1(1, [5], range(X_PASSES))
    turn(w2[2], 4)
    turn(w2[3], 0)
    for key, bank in zip(keys_a[:4], [2, 3, 6, 5]):
        mm2(key, bank, range(2))
    mm1(1, [6], range(X_PASSES))
    for key, bank in zip(keys_a[4:7], [7, 0, 1]):
        mm2(key, bank, range(2))
    for part in single:
        mm1(1, [7], range(X_PASSES), part)
    mm2(keys_a[7], 4, range(2))
    for key, bank in zip(keys_b, [7, 0, 1, 2, 3, 6, 5, 4]):
        mm2(key, bank, range(2))

    def widen(unit, tiles):
        return [("widen", unit, a) for a in tiles]

    def empty(unit):
        return [("empty", unit, 0), ("empty", unit, 1)]

    def split(unit):
        return [("split", unit, 0), ("split", unit, 1)]

    def relu(half, fs):
        return [("relu", half, f, whole) for f in fs]

    helped = [1, 1, 1, 1, 1, 1, 1, 1, 2, 2] + [0] * 6

    def own(i):
        return widen(stream[i], range(TILES - helped[i]))

    def aid(i):
        return widen(stream[i], range(TILES - helped[i], TILES))

    def sort(i):
        return [("sort_words", W1_CHUNKS[i]), ("sort_scales", W1_CHUNKS[i])]

    vector = [("fill_zeros",), ("fill_w1_scales",), ("fill_warm",), ("fill_b1",), ("unit_column",), ("sort_b1",)]
    vector += own(0) + [("empty_b1",)] + sort(0)[:1] + own(1) + sort(0)[1:] + [("quant", xa[0])]
    vector += sort(1) + own(2)[:1] + [("quant", xa[1])] + own(2)[1:]
    vector += own(3) + sort(2)[:1] + [("quant", xa[2])] + sort(2)[1:]
    vector += own(4) + own(5)[:1] + [("quant", xa[3])] + own(5)[1:] + sort(3) + [("quant", xa[4])]
    vector += own(6) + own(7)[:2] + [("quant", xa[5])] + own(7)[2:] + own(8) + own(9)[:1] + [("quant", xb[0])] + own(9)[1:] + own(10) + [("quant", xb[1])]
    vector += own(11) + [("quant", xb[2])] + own(12) + [("h_weave", 0, 0, whole), ("quant", xb[3]), ("quant", xb[4])] + own(13) + split(w2[0])[:1]
    vector += [("quant", xb[5])] + split(w2[0])[1:] + split(w2[1]) + own(14) + own(15) + [("h_quant", 0, 0, whole)] + split(w2[3]) + [("h_quant", 0, 1, whole), ("quant", w2[0])]
    vector += [("h_weave", 1, 0, (0, 2)), ("quant", w2[1]), ("h_weave", 1, 0, (2, 4)), ("quant", w2[2]), ("bias", keys_a[0]), ("bias", keys_a[1]), ("quant", w2[3]), ("bias", keys_a[2]), ("bias", keys_a[3]), ("h_quant", 1, 0, whole)]
    vector += [("bias", key) for key in keys_a[4:7]]
    vector += [("h_weave", 1, 1, single[0]), ("h_weave", 1, 1, single[1]), ("h_quant", 1, 1, single[0]), ("h_weave", 1, 1, single[2]), ("h_quant", 1, 1, single[1]), ("bias", keys_a[7])]
    vector += [("h_quant", 1, 1, single[2]), ("bias", keys_b[0]), ("h_quant", 1, 1, single[3])]
    vector += [("bias", key) for key in keys_b[1:]]

    scalar = [("warm_scalar",)] + aid(0) + empty(xa[0]) + aid(1) + empty(xa[1]) + aid(2)
    scalar += aid(3) + empty(xa[2]) + aid(4) + aid(5) + empty(xa[3]) + aid(6) + aid(7) + empty(xa[4]) + aid(8) + empty(xa[5]) + aid(9) + empty(xb[0])
    scalar += relu(0, [0, 1]) + empty(xb[1]) + relu(0, [2, 3, 4]) + empty(xb[2]) + relu(0, [5, 6, 7]) + empty(xb[3]) + empty(xb[4])
    scalar += [("h_weave", 0, 1, (0, 2))] + empty(xb[5]) + [("h_weave", 0, 1, (2, 4))]
    scalar += relu(1, [0, 1, 2, 3]) + split(w2[2])[:1] + empty(w2[0]) + split(w2[2])[1:] + empty(w2[1]) + relu(1, [4]) + empty(w2[2]) + empty(w2[3]) + relu(1, [5])
    scalar += [("tanh", key) for key in keys_a[0:3]] + relu(1, [6]) + [("tanh", key) for key in keys_a[3:5]]
    scalar += [("relu", 1, 7, single[0]), ("tanh", keys_a[5]), ("relu", 1, 7, single[1]), ("relu", 1, 7, single[2]), ("tanh", keys_a[6]), ("relu", 1, 7, single[3]), ("h_weave", 1, 1, single[3])]
    scalar += [("tanh", key) for key in keys_a[7:] + keys_b]

    sync = [("load_b1",), ("load_x_scale",), ("load_x", 0, X_CHUNKS[0][0]), ("load_w1", W1_CHUNKS[0]), ("load_x", 0, X_CHUNKS[0][1]), ("load_w1_scales", SCALE_CHUNKS[0])]
    sync += [("load_w1", W1_CHUNKS[1]), ("load_x", 0, X_CHUNKS[0][2]), ("load_w1_scales", SCALE_CHUNKS[1]), ("load_w1", W1_CHUNKS[2]), ("load_x", 0, X_CHUNKS[0][3]), ("load_w1", W1_CHUNKS[3])]
    sync += [("load_x", 1, c) for c in X_CHUNKS[1]] + [("load_w2_scale",), ("load_w2", 0), ("load_w2", 1), ("load_b2",)]
    sync += [("store", key) for key in keys_a + keys_b]
    return {"sync": sync, "gpsimd": [("identities",)], "vector": vector, "scalar": scalar, "tensor": tensor}, bank_of


def prerequisites(orders):
    needs = {}
    steps = [step for order in orders.values() for step in order]
    units = [step[1] for step in orders["tensor"] if step[0] == "turn" and step[2] == 0]
    results = [step[1] for step in orders["vector"] if step[0] == "bias"]
    parts = {}
    for step in steps:
        if step[0] == "h_quant":
            parts.setdefault(step[1:3], []).append(step[3])
    for step in steps:
        kind = step[0]
        before = []
        if kind == "widen":
            unit, a = step[1], step[2]
            if unit[0] == "x":
                before += [("load_x", unit[1], chunk_of(X_CHUNKS[unit[1]], unit[2])), ("load_x_scale",)]
            else:
                before += [("load_w2", unit[1]), ("load_w2_scale",)]
            if units.index(unit) >= WIDE_SLOTS:
                before.append(("turn", units[units.index(unit) - WIDE_SLOTS], a // 2))
        elif kind == "split":
            before += [("widen", step[1], 2 * step[2]), ("widen", step[1], 2 * step[2] + 1)]
        elif kind == "turn":
            before += [("widen", step[1], 2 * step[2]), ("widen", step[1], 2 * step[2] + 1), ("identities",)]
            if ("split",) + step[1:] in steps:
                before.append(("split",) + step[1:])
        elif kind == "empty":
            before.append(("turn", step[1], step[2]))
            if units.index(step[1]) >= WOVEN_SLOTS:
                before.append(("quant", units[units.index(step[1]) - WOVEN_SLOTS]))
        elif kind == "quant":
            before += [("empty", step[1], 0), ("empty", step[1], 1)]
        elif kind == "load_w1_scales":
            before.append(("fill_w1_scales",))
        elif kind == "warm_tensor":
            before.append(("fill_zeros",))
        elif kind == "warm_scalar":
            before.append(("fill_warm",))
        elif kind == "sort_b1":
            before += [("fill_b1",), ("load_b1",)]
        elif kind == "unit_column":
            before.append(("identities",))
        elif kind == "sort_words":
            before.append(("load_w1", step[1]))
        elif kind == "sort_scales":
            before.append(("load_w1_scales", chunk_of(SCALE_CHUNKS, step[1][0])))
        elif kind == "turn_b1":
            before += [("sort_b1",), ("unit_column",)]
        elif kind == "empty_b1":
            before.append(("turn_b1",))
        elif kind == "mm1":
            half, f, part, g = step[1:5]
            before += [("quant", ("x", half, g)), ("sort_words", chunk_of(W1_CHUNKS, g)), ("sort_scales", chunk_of(W1_CHUNKS, g))]
        elif kind == "relu":
            before += [("mm1",) + step[1:] + (X_PASSES - 1,), ("empty_b1",)]
        elif kind == "h_weave":
            before += [s for s in steps if s[:2] == ("relu", step[1]) and s[2] // 4 == step[2] and s[3][0] < step[3][1] and step[3][0] < s[3][1]]
        elif kind == "h_quant":
            before += [s for s in steps if s[:3] == ("h_weave",) + step[1:3] and s[3][0] < step[3][1] and step[3][0] < s[3][1]]
        elif kind == "mm2":
            (half, a, n), g = step[1], step[2]
            before.append(("quant", ("w", n, g)))
            before += [("h_quant", half, g, part) for part in parts[(half, g)] if part[0] <= a < part[1]]
        elif kind == "bias":
            before += [("mm2", step[1], H_PASSES - 1), ("load_b2",)]
            if results.index(step[1]) >= RESULT_SLOTS:
                before.append(("store", results[results.index(step[1]) - RESULT_SLOTS]))
        elif kind == "tanh":
            before.append(("bias", step[1]))
        elif kind == "store":
            before.append(("tanh", step[1]))
        needs[step] = before
    return needs, units, results


def tile_click_autoencoder_encoder_d6_kernel(
    tc, x_bytes, x_scale, w1_words, w1_scales, b1, w2_bytes, w2_scale, b2, out
):
    nc = tc.nc
    orders, bank_of = engine_orders()
    needs, units, results = prerequisites(orders)
    engine_of = {step: engine for engine, order in orders.items() for step in order}

    emptied_by = {}
    for step in orders["tensor"]:
        tenant = {"turn": ("empty",) + step[1:], "turn_b1": ("empty_b1",), "mm1": ("relu",) + step[1:4], "mm2": ("bias",) + step[1:2]}.get(step[0])
        if tenant is None:
            continue
        bank = bank_of[tenant]
        if emptied_by.get(bank, tenant) != tenant:
            needs[step].append(emptied_by[bank])
        emptied_by[bank] = tenant

    with ExitStack() as ctx:
        sbuf = ctx.enter_context(tc.tile_pool(name="sbuf", bufs=1))
        psum = ctx.enter_context(tc.psum_pool(name="psum", bufs=1))

        def alloc(name, shape, dtype):
            return sbuf.tile(shape, dtype, name=name, align_bytes=64)

        banks = [psum.tile([P, PASS], F32, name="bank%d" % b) for b in range(8)]
        x_raw = {
            (half, c): alloc("x_raw%d_%d" % (half, c[0]), [P, TILES, (c[1] - c[0]) * PASS], U8)
            for half in range(2)
            for c in X_CHUNKS[half]
        }
        w2_raw = [alloc("w2_raw%d" % n, [P, TILES, HIDDEN], U8) for n in range(2)]
        x_sc = alloc("x_sc", [P, 2 * TILES * (ITEMS // P)], F32)
        w2_sc = alloc("w2_sc", [P, 64], F32)
        w1_raw = {c: alloc("w1_raw%d" % c[0], [P, c[1] - c[0], 2 * HIDDEN], U8) for c in W1_CHUNKS}
        w1_sorted = alloc("w1_sorted", [P, X_PASSES, 2 * HIDDEN], U8)
        w1s_raw = alloc("w1s_raw", [P, X_PASSES, HIDDEN], U8)
        w1s_sorted = alloc("w1s_sorted", [P, X_PASSES, HIDDEN], U8)
        b1_raw = alloc("b1_raw", [1, HIDDEN], BF16)
        b1_rows = alloc("b1_rows", [P, HIDDEN], BF16)
        b1_cols = alloc("b1_cols", [P, 8], F32)
        b2_all = alloc("b2_all", [P, CODES], BF16)
        ident32 = alloc("ident32", [P, P], F32)
        unit_col = alloc("unit_col", [P, 2], BF16)
        warm = alloc("warm", [P, 16], F32)
        zeros = alloc("zeros", [P, PASS], BF16)
        wide = [alloc("wide%d" % s, [P, TILES, PASS], BF16) for s in range(WIDE_SLOTS)]
        w2_split = {s[1]: alloc("w2_split%d%d" % s[1][1:], [P, TILES, PASS], BF16) for s in engine_of if s[0] == "split" and s[2] == 0}
        woven = [alloc("woven%d" % s, [P, 4 * PASS], BF16) for s in range(WOVEN_SLOTS)]
        codes = {u: alloc("codes_%s%d%d" % u, [P, PASS], U32) for u in units}
        scales = {u: alloc("scales_%s%d%d" % u, [P, PASS], U8) for u in units}
        groups = [(half, g) for half in range(2) for g in range(H_PASSES)]
        h_planes = {k: alloc("h_planes%d%d" % k, [P, 4, PASS], BF16) for k in groups}
        h_woven = {k: alloc("h_woven%d%d" % k, [P, 4 * PASS], BF16) for k in groups}
        h_codes = {k: alloc("h_codes%d%d" % k, [P, PASS], U32) for k in groups}
        h_scales = {k: alloc("h_scales%d%d" % k, [P, PASS], U8) for k in groups}
        result = [alloc("result%d" % s, [P, PASS], F32) for s in range(RESULT_SLOTS)]

        x_rows = x_bytes.rearrange("(p a) k -> p a k", a=2 * TILES)
        out_rows = out.rearrange("(p a) n -> p a n", a=2 * TILES)

        def copy_on(engine, dst, src):
            if engine == "vector":
                nc.vector.tensor_copy(out=dst, in_=src)
            else:
                nc.scalar.copy(out=dst, in_=src)

        def run_step(step):
            kind = step[0]
            engine = engine_of[step]
            if kind == "load_x":
                half, c = step[1], step[2]
                nc.sync.dma_start(out=x_raw[(half, c)][:], in_=x_rows[:, TILES * half : TILES * (half + 1), c[0] * PASS : c[1] * PASS])
            elif kind == "load_x_scale":
                nc.sync.dma_start(out=x_sc[:], in_=x_scale.rearrange("(p a) j -> p (a j)", a=2 * TILES))
            elif kind == "load_w2":
                n = step[1]
                nc.sync.dma_start(out=w2_raw[n][:], in_=w2_bytes.rearrange("(i p) k -> p i k", p=P)[:, TILES * n : TILES * (n + 1), :])
            elif kind == "load_w2_scale":
                nc.sync.dma_start(out=w2_sc[:], in_=w2_scale.rearrange("i j -> (i j)").partition_broadcast(P))
            elif kind == "load_b2":
                nc.sync.dma_start(out=b2_all[:], in_=b2.partition_broadcast(P))
            elif kind == "load_w1":
                c = step[1]
                nc.sync.dma_start(out=w1_raw[c][:].bitcast(I32), in_=w1_words[c[0] : c[1]].rearrange("g p b -> p g b").bitcast(I32))
            elif kind == "fill_w1_scales":
                nc.vector.memset(w1s_raw[:].bitcast(I32), 0)
            elif kind == "load_w1_scales":
                c = step[1]
                for q in range(4):
                    nc.sync.dma_start(
                        out=w1s_raw[32 * q : 32 * q + 4, c[0] : c[1], :].bitcast(I32),
                        in_=w1_scales[c[0] : c[1], 4 * q : 4 * q + 4, :].rearrange("g r n -> r g n").bitcast(I32),
                    )
            elif kind == "fill_b1":
                nc.vector.memset(b1_rows[:].bitcast(I32), 0)
            elif kind == "load_b1":
                nc.sync.dma_start(out=b1_raw[:], in_=b1.rearrange("(o f) -> o f", o=1))
            elif kind == "sort_b1":
                nc.vector.tensor_copy(
                    out=b1_rows[0:1, :].rearrange("o (g t s w) -> o g t s w", g=H_PASSES, t=4, w=4),
                    in_=b1_raw[:].rearrange("o (g s t w) -> o g t s w", g=H_PASSES, t=4, w=4),
                )
            elif kind == "identities":
                make_identity(nc, ident32[:])
            elif kind == "unit_column":
                nc.vector.tensor_copy(out=unit_col[:], in_=ident32[:, 0:2])
            elif kind == "fill_warm":
                nc.vector.memset(warm[:, 0:8], 0.0)
            elif kind == "fill_zeros":
                nc.vector.memset(zeros[:].bitcast(I32), 0)
            elif kind == "warm_tensor":
                nc.tensor.matmul(banks[bank_of[step]][:], lhsT=zeros[:, 0:P], rhs=zeros[:], start=True, stop=True)
            elif kind == "warm_scalar":
                nc.scalar.activation(out=warm[:, 8:16], in_=warm[:, 0:8], func=ACT.Tanh)
            elif kind == "turn_b1":
                for f in range(8):
                    nc.tensor.matmul(banks[bank_of[("empty_b1",)]][:, 2 * f : 2 * f + 2], lhsT=b1_rows[:, f * P : (f + 1) * P], rhs=unit_col[:], start=True, stop=True)
            elif kind == "empty_b1":
                nc.vector.tensor_copy(out=b1_cols[:], in_=banks[bank_of[step]][:, 0:16:2])
            elif kind == "sort_words":
                c = step[1]
                src = w1_raw[c][:].bitcast(I32).rearrange("p g (h s t w) -> p (g h) t s w", h=H_PASSES, t=4, w=2)
                dst = w1_sorted[:, c[0] : c[1], :].bitcast(I32).rearrange("p g (h t s w) -> p (g h) t s w", h=H_PASSES, t=4, w=2)
                nc.vector.tensor_copy(out=dst, in_=src)
            elif kind == "sort_scales":
                c = step[1]
                src = w1s_raw[:, c[0] : c[1], :].bitcast(I32).rearrange("p g (h s t) -> p (g h) t s", h=H_PASSES, t=4)
                dst = w1s_sorted[:, c[0] : c[1], :].bitcast(I32).rearrange("p g (h t s) -> p (g h) t s", h=H_PASSES, t=4)
                nc.vector.tensor_copy(out=dst, in_=src)
            elif kind == "widen":
                unit, a = step[1], step[2]
                dst = wide[units.index(unit) % WIDE_SLOTS][:, a, :]
                for j in range(4):
                    if unit[0] == "x":
                        half, g = unit[1], unit[2]
                        c = chunk_of(X_CHUNKS[half], g)
                        k0 = (g - c[0]) * PASS + j * P
                        src = x_raw[(half, c)][:, a, k0 : k0 + P].bitcast(FP8)
                        col = (TILES * half + a) * (ITEMS // P) + 4 * g + j
                        scale = x_sc[:, col : col + 1]
                        if engine == "scalar":
                            nc.scalar.activation(out=dst[:, j * P : (j + 1) * P], in_=src, func=ACT.Copy, scale=scale)
                        else:
                            nc.vector.tensor_scalar(
                                out=dst.rearrange("p (u m e) -> p m u e", u=2, e=2)[:, 32 * j : 32 * (j + 1)],
                                in0=src.rearrange("p (m u e) -> p m u e", u=2, e=2),
                                scalar1=scale, scalar2=None, op0=ALU.mult,
                            )
                    else:
                        n, g = unit[1], unit[2]
                        src = w2_raw[n][:, a, g * PASS + j * P : g * PASS + (j + 1) * P].bitcast(FP8)
                        col = (TILES * n + a) * (HIDDEN // P) + 4 * g + j
                        nc.vector.tensor_scalar(
                            out=dst[:, j * P : (j + 1) * P].rearrange("p (s w t) -> p s t w", w=4, t=4),
                            in0=src.rearrange("p (s t w) -> p s t w", t=4, w=4),
                            scalar1=w2_sc[:, col : col + 1], scalar2=None, op0=ALU.mult,
                        )
            elif kind == "split":
                unit, pair = step[1], step[2]
                src = wide[units.index(unit) % WIDE_SLOTS][:, 2 * pair : 2 * pair + 2, :].bitcast(F32)
                dst = w2_split[unit][:, 2 * pair : 2 * pair + 2, :].bitcast(F32)
                copy_on(engine, dst.rearrange("p i (u m) -> p i u m", u=2), src.rearrange("p i (m u) -> p i u m", u=2))
            elif kind == "turn":
                unit, pair = step[1], step[2]
                bank = banks[bank_of[("empty", unit, pair)]]
                for i in range(2):
                    a = 2 * pair + i
                    words = wide[units.index(unit) % WIDE_SLOTS][:, a, :].bitcast(F32)
                    planar = unit[0] == "x" and engine_of[("widen", unit, a)] == "vector"
                    if ("split", unit, pair) in engine_of:
                        words, planar = w2_split[unit][:, a, :].bitcast(F32), True
                    for u in range(2):
                        src = words[:, u * P : (u + 1) * P] if planar else words[:, u : 2 * P : 2]
                        nc.tensor.transpose(bank[:, (2 * i + u) * P : (2 * i + u + 1) * P], src, ident32[:])
            elif kind == "empty":
                unit, pair = step[1], step[2]
                dst = woven[units.index(unit) % WOVEN_SLOTS][:].bitcast(F32)[:, pair * PASS : (pair + 1) * PASS]
                copy_on(engine, dst.rearrange("p (i r u) -> p i r u", i=2, u=2), banks[bank_of[step]][:].rearrange("p (i u r) -> p i r u", i=2, u=2))
            elif kind == "quant":
                unit = step[1]
                nc.vector.quantize_mx(out=codes[unit][:].bitcast(FP8X4), scales=scales[unit][:], in_=woven[units.index(unit) % WOVEN_SLOTS][:])
            elif kind == "mm1":
                half, f, part, g = step[1:5]
                cols = slice(part[0] * P, part[1] * P)
                nc.tensor.matmul_mx(
                    out=banks[bank_of[("relu", half, f, part)]][:, 0 : (part[1] - part[0]) * P],
                    lhsT=w1_sorted[:, g, 2 * P * f : 2 * P * (f + 1)].bitcast(FP4X4),
                    lhsT_scale=w1s_sorted[:, g, P * f : P * (f + 1)],
                    rhs=codes[("x", half, g)][:, cols].bitcast(FP8X4),
                    rhs_scale=scales[("x", half, g)][:, cols],
                    start=(g == 0), stop=(g == X_PASSES - 1),
                )
            elif kind == "relu":
                half, f, part = step[1:4]
                dst = h_planes[(half, f // 4)][:, f % 4, part[0] * P : part[1] * P]
                src = banks[bank_of[step]][:, 0 : (part[1] - part[0]) * P]
                if engine == "scalar":
                    nc.scalar.activation(out=dst, in_=src, func=ACT.Relu, bias=b1_cols[:, f : f + 1])
                else:
                    nc.vector.tensor_scalar(out=dst, in0=src, scalar1=b1_cols[:, f : f + 1], scalar2=0.0, op0=ALU.add, op1=ALU.max)
            elif kind == "h_weave":
                half, g, part = step[1:4]
                src = h_planes[(half, g)][:, :, part[0] * P : part[1] * P]
                dst = h_woven[(half, g)][:, 4 * part[0] * P : 4 * part[1] * P]
                copy_on(engine, dst.rearrange("p (c i t) -> p c t i", i=4, t=4), src.rearrange("p t (c i) -> p c t i", i=4))
            elif kind == "h_quant":
                half, g, part = step[1:4]
                cols = slice(part[0] * P, part[1] * P)
                nc.vector.quantize_mx(
                    out=h_codes[(half, g)][:, cols].bitcast(FP8X4),
                    scales=h_scales[(half, g)][:, cols],
                    in_=h_woven[(half, g)][:, 4 * part[0] * P : 4 * part[1] * P],
                )
            elif kind == "mm2":
                (half, a, n), g = step[1], step[2]
                nc.tensor.matmul_mx(
                    out=banks[bank_of[("bias", step[1])]][:],
                    lhsT=h_codes[(half, g)][:, a * P : (a + 1) * P].bitcast(FP8X4),
                    lhsT_scale=h_scales[(half, g)][:, a * P : (a + 1) * P],
                    rhs=codes[("w", n, g)][:].bitcast(FP8X4),
                    rhs_scale=scales[("w", n, g)][:],
                    start=(g == 0), stop=(g == H_PASSES - 1),
                )
            elif kind == "bias":
                n = step[1][2]
                nc.vector.tensor_tensor(
                    out=result[results.index(step[1]) % RESULT_SLOTS][:], in0=banks[bank_of[step]][:],
                    in1=b2_all[:, n * PASS : (n + 1) * PASS], op=ALU.add,
                )
            elif kind == "tanh":
                tile = result[results.index(step[1]) % RESULT_SLOTS]
                nc.scalar.activation(out=tile[:], in_=tile[:], func=ACT.Tanh)
            else:
                half, a, n = step[1]
                nc.sync.dma_start(
                    out=out_rows[:, TILES * half + a, n * PASS : (n + 1) * PASS],
                    in_=result[results.index(step[1]) % RESULT_SLOTS][:],
                )

        done = set()
        position = {engine: 0 for engine in orders}
        with tc.manual_schedule():
            while any(position[engine] < len(order) for engine, order in orders.items()):
                progress = False
                for engine, order in orders.items():
                    while position[engine] < len(order) and all(s in done for s in needs[order[position[engine]]]):
                        step = order[position[engine]]
                        run_step(step)
                        done.add(step)
                        position[engine] += 1
                        progress = True
                assert progress
